import numpy as np
import ml_dtypes


def mxq(x, axis, fmt="e4m3"):
    dtype, down = {"e4m3": (ml_dtypes.float8_e4m3fn, 7), "e5m2": (ml_dtypes.float8_e5m2, 14)}[fmt]
    v = np.moveaxis(np.asarray(x, np.float32).astype(ml_dtypes.bfloat16).astype(np.float64), axis, -1)
    blocks = v.reshape(v.shape[:-1] + (-1, 32))
    amax = np.abs(blocks).max(-1, keepdims=True)
    byte = np.maximum(np.where(amax > 0, np.frexp(amax)[1] - 1 + 127, 0) - down, 1)
    scale = np.exp2(byte - 127.0)
    codes = (blocks / scale).astype(np.float32).astype(dtype).astype(np.float64)
    return np.moveaxis((codes * scale).reshape(v.shape), -1, axis)


WIDE = False


def mx_kscale(k):
    if not WIDE:
        return np.ones(k)
    levels = np.array([30, -30])
    if k % 512:
        return np.exp2(np.random.permutation(np.resize(levels, k // 32))).repeat(32)
    a = np.empty((k // 512, 16))
    for p in range(k // 512):
        a[p, :8] = np.random.permutation(np.resize(levels, 8))
        for g in range(8):
            far = levels[np.abs(levels - a[p, g]) >= 10]
            a[p, g + 8] = far[np.random.randint(len(far))]
    return np.exp2(a.ravel()).repeat(32)


def f64(x):
    return np.asarray(x).astype(np.float64)


def striped(idx):
    return np.tile(np.asarray(idx).reshape(-1, 16).T, (8, 1)).astype(np.uint16)


def unstriped(offs):
    return offs[:16].T.reshape(-1).astype(np.int64)


def striped8(idx):
    return np.asarray(idx).reshape(8, -1, 16).transpose(0, 2, 1).reshape(128, -1).astype(np.uint16)


def unstriped8(offs):
    return offs.reshape(8, 16, -1).transpose(0, 2, 1).reshape(8, -1).astype(np.int64)


def pick8(x, idx, run):
    r = np.arange(len(x))
    return x[r[:, None], idx[r % (8 * run) // run]]


E2M1 = np.array([0.0, 0.5, 1.0, 1.5, 2.0, 3.0, 4.0, 6.0, -0.0, -0.5, -1.0, -1.5, -2.0, -3.0, -4.0, -6.0])


def pack_weight(w, fmt):
    k, n = w.shape
    w = f64(np.asarray(w, np.float32).astype(ml_dtypes.bfloat16)).reshape(k // 32, 32, n)
    amax = np.abs(w).max(1)
    if fmt in ("e4m3", "e5m2"):
        byte = np.frexp(amax)[1] - 1 + 127 - (7 if fmt == "e4m3" else 14)
    else:
        mant, ex = np.frexp(amax / 6.0)
        byte = np.where(mant > 0.5, ex, ex - 1) + 127
    byte = np.clip(np.where(amax > 0, byte, 1), 1, 254)
    scaled = (w * np.exp2(127.0 - byte)[:, None, :]).reshape(k, n).astype(np.float32)
    by_word = np.ascontiguousarray(scaled.reshape(k // 512, 128, 4, n).transpose(0, 1, 3, 2))
    if fmt in ("e4m3", "e5m2"):
        words = by_word.astype(ml_dtypes.float8_e4m3fn if fmt == "e4m3" else ml_dtypes.float8_e5m2).view(np.uint8)
    else:
        c = by_word.astype(ml_dtypes.float4_e2m1fn).view(np.uint8) & 0xF
        words = (c[..., 0::2] | (c[..., 1::2] << 4)).reshape(k // 512, 128, 2 * n)
    return np.ascontiguousarray(words), np.ascontiguousarray(byte.astype(np.uint8).reshape(k // 512, 16, n))


def unpack_weight(words, scales, fmt):
    g, _, n = scales.shape
    words = np.ascontiguousarray(words).reshape(g, 128, n, -1)
    if fmt in ("e4m3", "e5m2"):
        vals = words.view(ml_dtypes.float8_e4m3fn if fmt == "e4m3" else ml_dtypes.float8_e5m2).astype(np.float64)
    else:
        nib = np.empty((g, 128, n, 4), np.uint8)
        nib[..., 0::2] = words & 0xF
        nib[..., 1::2] = words >> 4
        vals = E2M1[nib]
    vals = vals * np.repeat(np.exp2(scales.astype(np.float64) - 127.0), 8, axis=1)[..., None]
    return vals.transpose(0, 1, 3, 2).reshape(g * 512, n)


K, T, J, R, F, Z, C, O, N, E = 512, 1024, 256, 512, 512, 1024, 512, 128, 256, 512


def setup_inputs():
    n = np.random.standard_normal
    idx = np.random.permutation(T)[:J]
    idx2 = np.random.permutation(Z)[:J]
    idx3 = np.stack([np.random.permutation(C)[:J] for _ in range(8)])
    idx4 = np.random.permutation(C)[:J]
    idx5 = np.random.permutation(J)[:O]
    idx6 = np.random.permutation(J)[:O]
    idx7 = np.stack([np.random.permutation(E)[:O] for _ in range(8)])
    fk = mx_kscale(K)
    ff = mx_kscale(F)
    fr = mx_kscale(R)
    xtp = pack_weight(n((K, T)) / fk[:, None], "e5m2")
    xop = pack_weight(n((F, Z)) / ff[:, None], "e4m3")
    wp = pack_weight(n((K, R)) * 1 / np.sqrt(K) * fk[:, None] * fr, "e2m1")
    w2p = pack_weight(n((K, R)) * 1 / np.sqrt(K) * fk[:, None] * fr, "e4m3")
    w0p = pack_weight(n((F, R)) * 1 / np.sqrt(F) * ff[:, None] * fr, "e4m3")
    wbp = pack_weight(n((R, N)) * 1 / np.sqrt(R) / fr[:, None], "e2m1")
    return {
        "xt_words": xtp[0],
        "xt_scales": xtp[1],
        "xo_words": xop[0],
        "xo_scales": xop[1],
        "w_words": wp[0],
        "w_scales": wp[1],
        "w2_words": w2p[0],
        "w2_scales": w2p[1],
        "w0_words": w0p[0],
        "w0_scales": w0p[1],
        "sa": (np.random.uniform(0.5, 1.6, (R, 1))).astype(np.float32),
        "sb": (np.random.uniform(0.5, 1.6, (R, 1))).astype(np.float32),
        "wb_words": wbp[0],
        "wb_scales": wbp[1],
        "offs": striped(idx),
        "offs2": striped(idx2),
        "offs3": striped8(idx3),
        "offs4": striped(idx4),
        "offs5": striped(idx5),
        "offs6": striped(idx6),
        "offs7": striped8(idx7),
    }


def reference(xt_words, xt_scales, xo_words, xo_scales, w_words, w_scales, w2_words, w2_scales, w0_words, w0_scales, sa, sb, wb_words, wb_scales, offs, offs2, offs3, offs4, offs5, offs6, offs7):
    idx = unstriped(offs)
    idx2 = unstriped(offs2)
    idx3 = unstriped8(offs3)
    idx4 = unstriped(offs4)
    idx5 = unstriped(offs5)
    idx6 = unstriped(offs6)
    idx7 = unstriped8(offs7)
    xtu = unpack_weight(xt_words, xt_scales, "e5m2")
    xou = unpack_weight(xo_words, xo_scales, "e4m3")
    wu = unpack_weight(w_words, w_scales, "e2m1")
    w2u = unpack_weight(w2_words, w2_scales, "e4m3")
    w0u = unpack_weight(w0_words, w0_scales, "e4m3")
    wbu = unpack_weight(wb_words, wb_scales, "e2m1")
    xtidxg = xtu[:, idx]
    a = wu.T @ xtidxg
    xoidx2g = xou[:, idx2]
    b = w2u.T @ xtidxg + w0u.T @ xoidx2g
    pw = np.zeros((R, C))
    pw[np.arange(R)[:, None], idx3[np.arange(R) % 512 // 64]] = a
    rb = np.maximum(pw[:, idx4] * f64(sa), b)
    hid = np.abs(rb[:, idx5] - rb[:, idx6] * f64(sb))
    hidq = mxq(hid, 0, "e4m3")
    p = wbu.T @ hidq
    y = np.zeros((N, E))
    y[np.arange(N)[:, None], idx7[np.arange(N) % 128 // 16]] = p
    return y

@@ -1,0 +1,232 @@
+from contextlib import ExitStack
+
+import concourse.mybir as mybir
+
+K, T, J, R, NF, Z, C, O, N, E = 512, 1024, 256, 512, 512, 1024, 512, 128, 256, 512
+FLOPS = 2 * (2 * K * R * J + NF * R * J + R * N * O)
+
+F32 = mybir.dt.float32
+BF16 = mybir.dt.bfloat16
+I32 = mybir.dt.int32
+U32 = mybir.dt.uint32
+U16 = mybir.dt.uint16
+U8 = mybir.dt.uint8
+E4 = mybir.dt.float8_e4m3fn_x4
+E5 = mybir.dt.float8_e5m2_x4
+E2 = mybir.dt.float4_e2m1fn_x4
+ALU = mybir.AluOpType
+COPY = mybir.ActivationFunctionType.Copy
+P = 128
+PACK = 4
+
+
+def tile_list_ownanswer_leaned_one_ownpage_kernel(
+    tc, xt_words, xt_scales, xo_words, xo_scales, w_words, w_scales, w2_words, w2_scales, w0_words, w0_scales,
+    sa, sb, wb_words, wb_scales, offs, offs2, offs3, offs4, offs5, offs6, offs7, out):
+    nc = tc.nc
+    with ExitStack() as ctx:
+        sb_pool = ctx.enter_context(tc.tile_pool(name="keep", bufs=1))
+        psum = ctx.enter_context(tc.psum_pool(name="psum", bufs=1))
+
+        def sbuf(name, shape, dtype, tag=""):
+            return sb_pool.tile(shape, dtype, name=name, tag=tag or name, align_bytes=64)
+
+        def load_list(name, src):
+            lst = sb_pool.tile(list(src.shape), U16, name=name)
+            nc.sync.dma_start(lst[:], src)
+            return lst
+
+        def plane(name, cols):
+            pl = sbuf(name, [P, cols], U8)
+            nc.vector.memset(pl[:].bitcast(I32), 0)
+            return pl
+
+        def load_plane(pl, src, queue):
+            for q in range(4):
+                queue.dma_start(pl[32 * q:32 * q + 4, :].bitcast(I32), src[0, 4 * q:4 * q + 4, :].bitcast(I32))
+
+        def folded(name, cols):
+            pl = sbuf(name, [P, 2 * cols], U8)
+            nc.vector.memset(pl[0:64, :].bitcast(I32), 0)
+            return pl
+
+        def load_folded(pl, src):
+            rows = src[0].bitcast(I32).rearrange("(u q r) c -> q r u c", u=2, q=2)
+            for q in range(2):
+                nc.sync.dma_start(pl[32 * q:32 * q + 4, :].bitcast(I32).rearrange("r (u c) -> r u c", u=2), rows[q])
+
+        def unfold(pl):
+            cols = pl.shape[1] // 2
+            nc.vector.tensor_copy(pl[64:128, 0:cols].bitcast(I32), pl[0:64, cols:2 * cols].bitcast(I32))
+
+        def load_words(name, src, nbytes, queue=nc.sync):
+            tl = sbuf(name, [P, nbytes // 4], I32)
+            queue.dma_start(tl[:], src.bitcast(I32))
+            return tl
+
+        def flat(words):
+            return words[0].rearrange("p n t -> p (n t)")
+
+        w_w = load_words("w_w", w_words[0], 2 * R, nc.gpsimd)
+        xt_pl = plane("xt_pl", T)
+        w_pl = folded("w_pl", R)
+        xo_pl = plane("xo_pl", Z)
+        w2_pl = folded("w2_pl", R)
+        w0_pl = folded("w0_pl", R)
+        wb_pl = folded("wb_pl", N)
+        board = [sbuf("board%d" % i, [P, C], F32) for i in range(2)]
+        for bd in board:
+            nc.gpsimd.memset(bd[:], 0.0)
+
+        l1 = load_list("l1", offs)
+        xt_w = load_words("xt_w", flat(xt_words), 4 * T)
+        load_plane(xt_pl, xt_scales, nc.scalar)
+        load_folded(w_pl, w_scales)
+        l3 = load_list("l3", offs3)
+        l4 = load_list("l4", offs4)
+        sa_t = sbuf("sa_t", [P, PACK], F32)
+        nc.sync.dma_start(sa_t[:], sa.rearrange("(p t) o -> p (t o)", t=PACK))
+        l2 = load_list("l2", offs2)
+        load_plane(xo_pl, xo_scales, nc.sync)
+        xo_w = load_words("xo_w", flat(xo_words), 4 * Z)
+        load_folded(w2_pl, w2_scales)
+        load_folded(w0_pl, w0_scales)
+        w2_w = load_words("w2_w", flat(w2_words), 4 * R)
+        w0_w = load_words("w0_w", flat(w0_words), 4 * R)
+        l5 = load_list("l5", offs5)
+        l6 = load_list("l6", offs6)
+        sb_t = sbuf("sb_t", [P, PACK], F32)
+        nc.sync.dma_start(sb_t[:], sb.rearrange("(p t) o -> p (t o)", t=PACK))
+        load_folded(wb_pl, wb_scales)
+        wb_w = load_words("wb_w", wb_words[0], 2 * N)
+        l7 = load_list("l7", offs7)
+
+        xt_gs = sbuf("xt_gs", [P, J], U8)
+        xt_g = sbuf("xt_g", [P, J], U32)
+        HALF = J // 2
+
+        def half_cols(h):
+            return slice(HALF * h, HALF * (h + 1))
+
+        def half_list(lst, h):
+            return lst[:, HALF // 16 * h:HALF // 16 * (h + 1)]
+
+        def pick_scales(h):
+            nc.vector.tensor_copy(xt_gs[:, half_cols(h)], xt_pl[:].indirect(half_list(l1, h)))
+
+        def pick_words(h):
+            nc.vector.tensor_copy(xt_g[:, half_cols(h)], xt_w[:].bitcast(U32).indirect(half_list(l1, h)))
+
+        w_d = [sbuf("w_d%d" % t, [P, P], U16) for t in range(PACK)]
+        w_ds = [sbuf("w_ds%d" % t, [P, P], U8) for t in range(PACK)]
+
+        def deal_w(t):
+            nc.vector.tensor_copy(w_d[t][:], w_w[:].bitcast(U16)[:, t::PACK])
+            nc.vector.tensor_copy(w_ds[t][:], w_pl[:, t:R:PACK])
+
+        a_sb = [sbuf("a_sb%d" % t, [P, J], F32) for t in range(PACK)]
+
+        def first(t, cols, bank, copy):
+            a_ps = psum.tile([P, cols.stop - cols.start], F32, name="a_ps", tag="bank%d" % bank)
+            nc.tensor.matmul_mx(a_ps[:], lhsT=w_d[t][:].bitcast(E2), lhsT_scale=w_ds[t][:],
+                                rhs=xt_g[:, cols].bitcast(E5), rhs_scale=xt_gs[:, cols], start=True, stop=True)
+            copy(a_sb[t][:, cols], a_ps[:])
+
+        def put_half(t, h):
+            nc.scalar.activation(board[t % 2][:].indirect(half_list(l3, h)), a_sb[t][:, half_cols(h)], COPY)
+
+        pick_scales(0)
+        unfold(w_pl)
+        pick_words(0)
+        deal_w(0)
+        first(0, half_cols(0), 0, nc.scalar.copy)
+        put_half(0, 0)
+        deal_w(1)
+        first(1, half_cols(0), 1, nc.vector.tensor_copy)
+        put_half(1, 0)
+        pick_scales(1)
+        pick_words(1)
+        first(0, half_cols(1), 2, nc.vector.tensor_copy)
+        put_half(0, 1)
+        first(1, half_cols(1), 3, nc.vector.tensor_copy)
+        put_half(1, 1)
+        for t in range(2, PACK):
+            deal_w(t)
+            first(t, slice(0, J), t - 2, nc.vector.tensor_copy)
+
+        xo_gs = sbuf("xo_gs", [P, J], U8)
+        nc.vector.tensor_copy(xo_gs[:], xo_pl[:].indirect(l2[:]))
+        xo_g = sbuf("xo_g", [P, J], U32)
+        nc.vector.tensor_copy(xo_g[:], xo_w[:].bitcast(U32).indirect(l2[:]))
+
+        def deal(name, words, pl):
+            d = sbuf(name + "_d", [P, PACK, P], I32)
+            ds = sbuf(name + "_ds", [P, PACK, P], U8)
+            unfold(pl)
+            nc.vector.tensor_copy(d[:], words[:].rearrange("p (m t) -> p t m", t=PACK))
+            nc.vector.tensor_copy(ds[:], pl[:, 0:R].rearrange("p (m t) -> p t m", t=PACK))
+            return d, ds
+
+        w2_d, w2_ds = deal("w2", w2_w, w2_pl)
+        w0_d, w0_ds = deal("w0", w0_w, w0_pl)
+        b_ps = [psum.tile([P, J], F32, name="b_ps%d" % t, tag="bank%d" % (4 + t)) for t in range(PACK)]
+        for t in range(PACK):
+            nc.tensor.matmul_mx(b_ps[t][:], lhsT=w2_d[:, t, :].bitcast(E4), lhsT_scale=w2_ds[:, t, :],
+                                rhs=xt_g[:].bitcast(E5), rhs_scale=xt_gs[:], start=True, stop=False)
+            nc.tensor.matmul_mx(b_ps[t][:], lhsT=w0_d[:, t, :].bitcast(E4), lhsT_scale=w0_ds[:, t, :],
+                                rhs=xo_g[:].bitcast(E4), rhs_scale=xo_gs[:], start=False, stop=True)
+
+        unfold(wb_pl)
+        pages = [sbuf("page%d" % i, [P, E], F32, tag) for i, tag in enumerate(("xo_w", "w2_w"))]
+        for pg in pages:
+            nc.gpsimd.memset(pg[:], 0.0)
+
+        look = [sbuf("look%d" % t, [P, J], F32) for t in range(PACK)]
+        rb = [sbuf("rb%d" % t, [P, J], F32) for t in range(PACK)]
+        plain = sbuf("plain", [P, PACK, O], F32)
+        leaned = sbuf("leaned", [P, PACK, O], F32)
+        diff = sbuf("diff", [P, PACK, O], F32)
+        hid = sbuf("hid", [P, O, PACK], BF16)
+
+        def put(t):
+            nc.scalar.activation(board[t % 2][:].indirect(l3[:]), a_sb[t][:], COPY)
+
+        def fetch(t):
+            nc.scalar.activation(look[t][:], board[t % 2][:].indirect(l4[:]), COPY, scale=sa_t[:, t:t + 1])
+            nc.vector.tensor_tensor(rb[t][:], look[t][:], b_ps[t][:], ALU.max)
+            nc.vector.tensor_copy(plain[:, t, :], rb[t][:].indirect(l5[:]))
+
+        def lean(t):
+            nc.scalar.activation(leaned[:, t, :], rb[t][:].indirect(l6[:]), COPY, scale=sb_t[:, t:t + 1])
+
+        def magnitude(t0):
+            pair = slice(t0, t0 + 2)
+            nc.vector.tensor_tensor(diff[:, pair, :], plain[:, pair, :], leaned[:, pair, :], ALU.subtract)
+            dv = diff[:, pair, :].rearrange("p t o -> p o t")
+            nc.vector.scalar_tensor_tensor(hid[:, :, pair], dv, -1.0, dv, ALU.mult, ALU.max)
+
+        fetch(0)
+        put(2)
+        fetch(1)
+        put(3)
+        lean(0)
+        fetch(2)
+        lean(1)
+        magnitude(0)
+        fetch(3)
+        lean(2)
+        lean(3)
+        magnitude(2)
+
+        hq = sbuf("hq", [P, O], U32)
+        hs = sbuf("hs", [P, O], U8)
+        nc.vector.quantize_mx(hq[:].bitcast(E4), hs[:], hid[:].rearrange("p o t -> p (o t)"))
+        for i in range(2):
+            p_ps = psum.tile([P, O], F32, name="p_ps%d" % i, tag="bank%d" % i)
+            nc.tensor.matmul_mx(p_ps[:], lhsT=wb_w[:].bitcast(U8)[:, 2 * P * i:2 * P * (i + 1)].bitcast(E2),
+                                lhsT_scale=wb_pl[:, P * i:P * (i + 1)], rhs=hq[:].bitcast(E4), rhs_scale=hs[:],
+                                start=True, stop=True)
+            p_sb = sbuf("p_sb%d" % i, [P, O], F32)
+            nc.vector.tensor_copy(p_sb[:], p_ps[:])
+            nc.scalar.activation(pages[i][:].indirect(l7[:]), p_sb[:], COPY)
+            nc.sync.dma_start(out[P * i:P * (i + 1), :], pages[i][:])

@@ -36,69 +36,68 @@ def tile_list_ownanswer_leaned_one_ownpage_kernel(
             nc.sync.dma_start(lst[:], src)
             return lst
 
-        def plane(name, cols):
+        def plane(name, cols, engine=nc.vector):
             pl = sbuf(name, [P, cols], U8)
-            nc.vector.memset(pl[:].bitcast(I32), 0)
+            engine.memset(pl[:].bitcast(I32), 0)
             return pl
 
-        def load_plane(pl, src, queue):
+        def load_plane(pl, src, queues):
             for q in range(4):
-                queue.dma_start(pl[32 * q:32 * q + 4, :].bitcast(I32), src[0, 4 * q:4 * q + 4, :].bitcast(I32))
+                queues[q].dma_start(pl[32 * q:32 * q + 4, :].bitcast(I32), src[0, 4 * q:4 * q + 4, :].bitcast(I32))
 
-        def folded(name, cols):
+        def folded(name, cols, engine=nc.vector):
             pl = sbuf(name, [P, 2 * cols], U8)
-            nc.vector.memset(pl[0:64, :].bitcast(I32), 0)
+            engine.memset(pl[0:64, :].bitcast(I32), 0)
             return pl
 
-        def load_folded(pl, src):
+        def load_folded(pl, src, queue=nc.sync, row=0):
             rows = src[0].bitcast(I32).rearrange("(u q r) c -> q r u c", u=2, q=2)
             for q in range(2):
-                nc.sync.dma_start(pl[32 * q:32 * q + 4, :].bitcast(I32).rearrange("r (u c) -> r u c", u=2), rows[q])
+                queue.dma_start(pl[32 * q + row:32 * q + row + 4, :].bitcast(I32).rearrange("r (u c) -> r u c", u=2), rows[q])
 
         def unfold(pl):
             cols = pl.shape[1] // 2
             nc.vector.tensor_copy(pl[64:128, 0:cols].bitcast(I32), pl[0:64, cols:2 * cols].bitcast(I32))
 
-        def load_words(name, src, nbytes, queue=nc.sync):
+        def load_words(name, src, nbytes):
             tl = sbuf(name, [P, nbytes // 4], I32)
-            queue.dma_start(tl[:], src.bitcast(I32))
+            nc.sync.dma_start(tl[:], src.bitcast(I32))
             return tl
 
         def flat(words):
             return words[0].rearrange("p n t -> p (n t)")
 
-        w_w = load_words("w_w", w_words[0], 2 * R, nc.gpsimd)
+        w_pl = folded("w_pl", R, nc.gpsimd)
         xt_pl = plane("xt_pl", T)
-        w_pl = folded("w_pl", R)
         xo_pl = plane("xo_pl", Z)
-        w2_pl = folded("w2_pl", R)
-        w0_pl = folded("w0_pl", R)
-        wb_pl = folded("wb_pl", N)
+        b_pl = folded("b_pl", R)
+        wb_pl = plane("wb_pl", N)
         board = [sbuf("board%d" % i, [P, C], F32) for i in range(2)]
         for bd in board:
             nc.gpsimd.memset(bd[:], 0.0)
 
         l1 = load_list("l1", offs)
+        w_w = load_words("w_w", w_words[0], 2 * R)
         xt_w = load_words("xt_w", flat(xt_words), 4 * T)
-        load_plane(xt_pl, xt_scales, nc.scalar)
-        load_folded(w_pl, w_scales)
+        load_folded(w_pl, w_scales, nc.scalar)
+        load_plane(xt_pl, xt_scales, [nc.scalar, nc.scalar, nc.sync, nc.sync])
         l3 = load_list("l3", offs3)
+        l2 = load_list("l2", offs2)
+        load_plane(xo_pl, xo_scales, [nc.sync] * 4)
+        xo_w = load_words("xo_w", flat(xo_words), 4 * Z)
+        w2_w = load_words("w2_w", flat(w2_words), 4 * R)
+        w0_w = load_words("w0_w", flat(w0_words), 4 * R)
+        load_folded(b_pl, w2_scales)
+        load_folded(b_pl, w0_scales, row=4)
         l4 = load_list("l4", offs4)
         sa_t = sbuf("sa_t", [P, PACK], F32)
         nc.sync.dma_start(sa_t[:], sa.rearrange("(p t) o -> p (t o)", t=PACK))
-        l2 = load_list("l2", offs2)
-        load_plane(xo_pl, xo_scales, nc.sync)
-        xo_w = load_words("xo_w", flat(xo_words), 4 * Z)
-        load_folded(w2_pl, w2_scales)
-        load_folded(w0_pl, w0_scales)
-        w2_w = load_words("w2_w", flat(w2_words), 4 * R)
-        w0_w = load_words("w0_w", flat(w0_words), 4 * R)
         l5 = load_list("l5", offs5)
         l6 = load_list("l6", offs6)
         sb_t = sbuf("sb_t", [P, PACK], F32)
         nc.sync.dma_start(sb_t[:], sb.rearrange("(p t) o -> p (t o)", t=PACK))
-        load_folded(wb_pl, wb_scales)
         wb_w = load_words("wb_w", wb_words[0], 2 * N)
+        load_plane(wb_pl, wb_scales, [nc.sync] * 4)
         l7 = load_list("l7", offs7)
 
         xt_gs = sbuf("xt_gs", [P, J], U8)
@@ -117,31 +116,27 @@ def tile_list_ownanswer_leaned_one_ownpage_kernel(
         def pick_words(h):
             nc.vector.tensor_copy(xt_g[:, half_cols(h)], xt_w[:].bitcast(U32).indirect(half_list(l1, h)))
 
-        w_d = [sbuf("w_d%d" % t, [P, P], U16) for t in range(PACK)]
-        w_ds = [sbuf("w_ds%d" % t, [P, P], U8) for t in range(PACK)]
-
-        def deal_w(t):
-            nc.vector.tensor_copy(w_d[t][:], w_w[:].bitcast(U16)[:, t::PACK])
-            nc.vector.tensor_copy(w_ds[t][:], w_pl[:, t:R:PACK])
+        w_d = sbuf("w_d", [P, PACK, P], U16)
+        w_ds = sbuf("w_ds", [P, PACK, P], U8)
+        nc.scalar.copy(w_d[:], w_w[:].bitcast(U16).rearrange("p (m t) -> p t m", t=PACK))
+        unfold(w_pl)
+        nc.vector.tensor_copy(w_ds[:], w_pl[:, 0:R].rearrange("p (m t) -> p t m", t=PACK))
 
         a_sb = [sbuf("a_sb%d" % t, [P, J], F32) for t in range(PACK)]
 
         def first(t, cols, bank, copy):
             a_ps = psum.tile([P, cols.stop - cols.start], F32, name="a_ps", tag="bank%d" % bank)
-            nc.tensor.matmul_mx(a_ps[:], lhsT=w_d[t][:].bitcast(E2), lhsT_scale=w_ds[t][:],
+            nc.tensor.matmul_mx(a_ps[:], lhsT=w_d[:, t, :].bitcast(E2), lhsT_scale=w_ds[:, t, :],
                                 rhs=xt_g[:, cols].bitcast(E5), rhs_scale=xt_gs[:, cols], start=True, stop=True)
             copy(a_sb[t][:, cols], a_ps[:])
 
         def put_half(t, h):
             nc.scalar.activation(board[t % 2][:].indirect(half_list(l3, h)), a_sb[t][:, half_cols(h)], COPY)
 
-        pick_scales(0)
-        unfold(w_pl)
         pick_words(0)
-        deal_w(0)
+        pick_scales(0)
         first(0, half_cols(0), 0, nc.scalar.copy)
         put_half(0, 0)
-        deal_w(1)
         first(1, half_cols(0), 1, nc.vector.tensor_copy)
         put_half(1, 0)
         pick_scales(1)
@@ -151,7 +146,6 @@ def tile_list_ownanswer_leaned_one_ownpage_kernel(
         first(1, half_cols(1), 3, nc.vector.tensor_copy)
         put_half(1, 1)
         for t in range(2, PACK):
-            deal_w(t)
             first(t, slice(0, J), t - 2, nc.vector.tensor_copy)
 
         xo_gs = sbuf("xo_gs", [P, J], U8)
@@ -159,24 +153,23 @@ def tile_list_ownanswer_leaned_one_ownpage_kernel(
         xo_g = sbuf("xo_g", [P, J], U32)
         nc.vector.tensor_copy(xo_g[:], xo_w[:].bitcast(U32).indirect(l2[:]))
 
-        def deal(name, words, pl):
+        def deal(name, words):
             d = sbuf(name + "_d", [P, PACK, P], I32)
-            ds = sbuf(name + "_ds", [P, PACK, P], U8)
-            unfold(pl)
             nc.vector.tensor_copy(d[:], words[:].rearrange("p (m t) -> p t m", t=PACK))
-            nc.vector.tensor_copy(ds[:], pl[:, 0:R].rearrange("p (m t) -> p t m", t=PACK))
-            return d, ds
+            return d
 
-        w2_d, w2_ds = deal("w2", w2_w, w2_pl)
-        w0_d, w0_ds = deal("w0", w0_w, w0_pl)
+        w2_d = deal("w2", w2_w)
+        w0_d = deal("w0", w0_w)
+        unfold(b_pl)
+        b_ds = sbuf("b_ds", [P, PACK, P], U8)
+        nc.vector.tensor_copy(b_ds[:], b_pl[:, 0:R].rearrange("p (m t) -> p t m", t=PACK))
         b_ps = [psum.tile([P, J], F32, name="b_ps%d" % t, tag="bank%d" % (4 + t)) for t in range(PACK)]
         for t in range(PACK):
-            nc.tensor.matmul_mx(b_ps[t][:], lhsT=w2_d[:, t, :].bitcast(E4), lhsT_scale=w2_ds[:, t, :],
+            nc.tensor.matmul_mx(b_ps[t][:], lhsT=w2_d[:, t, :].bitcast(E4), lhsT_scale=b_ds[:, t, :],
                                 rhs=xt_g[:].bitcast(E5), rhs_scale=xt_gs[:], start=True, stop=False)
-            nc.tensor.matmul_mx(b_ps[t][:], lhsT=w0_d[:, t, :].bitcast(E4), lhsT_scale=w0_ds[:, t, :],
+            nc.tensor.matmul_mx(b_ps[t][:], lhsT=w0_d[:, t, :].bitcast(E4), lhsT_scale=b_ds[4:P, t, :],
                                 rhs=xo_g[:].bitcast(E4), rhs_scale=xo_gs[:], start=False, stop=True)
 
-        unfold(wb_pl)
         pages = [sbuf("page%d" % i, [P, E], F32, tag) for i, tag in enumerate(("xo_w", "w2_w"))]
         for pg in pages:
             nc.gpsimd.memset(pg[:], 0.0)

@@ -16,6 +16,7 @@ E5 = mybir.dt.float8_e5m2_x4
 E2 = mybir.dt.float4_e2m1fn_x4
 ALU = mybir.AluOpType
 COPY = mybir.ActivationFunctionType.Copy
+ABS = mybir.ActivationFunctionType.Abs
 P = 128
 PACK = 4
 
@@ -117,16 +118,20 @@ def tile_list_ownanswer_leaned_one_ownpage_kernel(
             nc.vector.tensor_copy(xt_g[:, half_cols(h)], xt_w[:].bitcast(U32).indirect(half_list(l1, h)))
 
         w_d = sbuf("w_d", [P, PACK, P], U16)
-        w_ds = sbuf("w_ds", [P, PACK, P], U8)
+        w_ds = [sbuf("w_ds0", [P, 2, P], U8), sbuf("w_ds1", [P, 2, P], U8, "xt_pl")]
+
+        def deal_w_scales(u):
+            nc.vector.tensor_copy(w_ds[u][:], w_pl[:, 0:R].rearrange("p (m t) -> p t m", t=PACK)[:, 2 * u:2 * u + 2, :])
+
         nc.scalar.copy(w_d[:], w_w[:].bitcast(U16).rearrange("p (m t) -> p t m", t=PACK))
         unfold(w_pl)
-        nc.vector.tensor_copy(w_ds[:], w_pl[:, 0:R].rearrange("p (m t) -> p t m", t=PACK))
+        deal_w_scales(0)
 
         a_sb = [sbuf("a_sb%d" % t, [P, J], F32) for t in range(PACK)]
 
         def first(t, cols, bank, copy):
             a_ps = psum.tile([P, cols.stop - cols.start], F32, name="a_ps", tag="bank%d" % bank)
-            nc.tensor.matmul_mx(a_ps[:], lhsT=w_d[:, t, :].bitcast(E2), lhsT_scale=w_ds[:, t, :],
+            nc.tensor.matmul_mx(a_ps[:], lhsT=w_d[:, t, :].bitcast(E2), lhsT_scale=w_ds[t // 2][:, t % 2, :],
                                 rhs=xt_g[:, cols].bitcast(E5), rhs_scale=xt_gs[:, cols], start=True, stop=True)
             copy(a_sb[t][:, cols], a_ps[:])
 
@@ -139,12 +144,13 @@ def tile_list_ownanswer_leaned_one_ownpage_kernel(
         put_half(0, 0)
         first(1, half_cols(0), 1, nc.vector.tensor_copy)
         put_half(1, 0)
-        pick_scales(1)
         pick_words(1)
+        pick_scales(1)
         first(0, half_cols(1), 2, nc.vector.tensor_copy)
         put_half(0, 1)
         first(1, half_cols(1), 3, nc.vector.tensor_copy)
         put_half(1, 1)
+        deal_w_scales(1)
         for t in range(2, PACK):
             first(t, slice(0, J), t - 2, nc.vector.tensor_copy)
 
@@ -178,48 +184,58 @@ def tile_list_ownanswer_leaned_one_ownpage_kernel(
         rb = [sbuf("rb%d" % t, [P, J], F32) for t in range(PACK)]
         plain = sbuf("plain", [P, PACK, O], F32)
         leaned = sbuf("leaned", [P, PACK, O], F32)
-        diff = sbuf("diff", [P, PACK, O], F32)
-        hid = sbuf("hid", [P, O, PACK], BF16)
+        OH = O // 2
+
+        def places(h):
+            return slice(OH * h, OH * (h + 1))
+
+        def place_list(lst, h):
+            return lst[:, OH // 16 * h:OH // 16 * (h + 1)]
 
         def put(t):
             nc.scalar.activation(board[t % 2][:].indirect(l3[:]), a_sb[t][:], COPY)
 
-        def fetch(t):
-            nc.scalar.activation(look[t][:], board[t % 2][:].indirect(l4[:]), COPY, scale=sa_t[:, t:t + 1])
-            nc.vector.tensor_tensor(rb[t][:], look[t][:], b_ps[t][:], ALU.max)
-            nc.vector.tensor_copy(plain[:, t, :], rb[t][:].indirect(l5[:]))
+        def fetch(t, cols=slice(0, J)):
+            offsets = l4[:, cols.start // 16:cols.stop // 16]
+            nc.scalar.activation(look[t][:, cols], board[t % 2][:].indirect(offsets), COPY, scale=sa_t[:, t:t + 1])
+            nc.vector.tensor_tensor(rb[t][:, cols], look[t][:, cols], b_ps[t][:, cols], ALU.max)
 
-        def lean(t):
-            nc.scalar.activation(leaned[:, t, :], rb[t][:].indirect(l6[:]), COPY, scale=sb_t[:, t:t + 1])
-
-        def magnitude(t0):
-            pair = slice(t0, t0 + 2)
-            nc.vector.tensor_tensor(diff[:, pair, :], plain[:, pair, :], leaned[:, pair, :], ALU.subtract)
-            dv = diff[:, pair, :].rearrange("p t o -> p o t")
-            nc.vector.scalar_tensor_tensor(hid[:, :, pair], dv, -1.0, dv, ALU.mult, ALU.max)
+        def pick(t, cols, offsets5, offsets6):
+            nc.scalar.activation(leaned[:, t, cols], rb[t][:].indirect(offsets6), COPY, scale=sb_t[:, t:t + 1])
+            nc.vector.tensor_copy(plain[:, t, cols], rb[t][:].indirect(offsets5))
 
         fetch(0)
-        put(2)
         fetch(1)
+        put(2)
         put(3)
-        lean(0)
         fetch(2)
-        lean(1)
-        magnitude(0)
-        fetch(3)
-        lean(2)
-        lean(3)
-        magnitude(2)
+        fetch(3, half_cols(0))
+        fetch(3, half_cols(1))
+        for t in range(PACK - 1):
+            pick(t, slice(0, O), l5[:], l6[:])
+        for h in range(2):
+            pick(PACK - 1, places(h), place_list(l5, h), place_list(l6, h))
 
-        hq = sbuf("hq", [P, O], U32)
-        hs = sbuf("hs", [P, O], U8)
-        nc.vector.quantize_mx(hq[:].bitcast(E4), hs[:], hid[:].rearrange("p o t -> p (o t)"))
+        hq = sbuf("hq", [P, 3 * OH], U32)
+        hs = sbuf("hs", [P, 3 * OH], U8)
+        nc.vector.memset(hq[:, OH:2 * OH].bitcast(I32), 0)
+        nc.vector.memset(hs[:, OH:2 * OH].bitcast(I32), 0)
+        diff = [sbuf("diff%d" % h, [P, PACK, OH], F32) for h in range(2)]
+        hid = [sbuf("hid%d" % h, [P, OH, PACK], BF16) for h in range(2)]
+        for h in range(2):
+            nc.vector.tensor_tensor(diff[h][:], plain[:, :, places(h)], leaned[:, :, places(h)], ALU.subtract)
+            nc.scalar.activation(hid[h][:], diff[h][:].rearrange("p t o -> p o t"), ABS)
+        for h in range(2):
+            made = slice(2 * OH * h, 2 * OH * h + OH)
+            read = slice(OH * h, OH * h + O)
+            nc.vector.quantize_mx(hq[:, made].bitcast(E4), hs[:, made], hid[h][:].rearrange("p o t -> p (o t)"))
+            for i in range(2):
+                p_ps = psum.tile([P, O], F32, name="p_ps", tag="bank%d" % (2 * h + i))
+                nc.tensor.matmul_mx(p_ps[:], lhsT=wb_w[:].bitcast(U8)[:, 2 * P * i:2 * P * (i + 1)].bitcast(E2),
+                                    lhsT_scale=wb_pl[:, P * i:P * (i + 1)], rhs=hq[:, read].bitcast(E4), rhs_scale=hs[:, read],
+                                    start=True, stop=True)
+                p_sb = sbuf("p_sb%d%d" % (h, i), [P, OH], F32)
+                nc.vector.tensor_copy(p_sb[:], p_ps[:, places(h)])
+                nc.scalar.activation(pages[i][:].indirect(place_list(l7, h)), p_sb[:], COPY)
         for i in range(2):
-            p_ps = psum.tile([P, O], F32, name="p_ps%d" % i, tag="bank%d" % i)
-            nc.tensor.matmul_mx(p_ps[:], lhsT=wb_w[:].bitcast(U8)[:, 2 * P * i:2 * P * (i + 1)].bitcast(E2),
-                                lhsT_scale=wb_pl[:, P * i:P * (i + 1)], rhs=hq[:].bitcast(E4), rhs_scale=hs[:],
-                                start=True, stop=True)
-            p_sb = sbuf("p_sb%d" % i, [P, O], F32)
-            nc.vector.tensor_copy(p_sb[:], p_ps[:])
-            nc.scalar.activation(pages[i][:].indirect(l7[:]), p_sb[:], COPY)
             nc.sync.dma_start(out[P * i:P * (i + 1), :], pages[i][:])

from contextlib import ExitStack

import concourse.mybir as mybir

K, T, J, R, NF, Z, C, O, N, E = 512, 1024, 256, 512, 512, 1024, 512, 128, 256, 512
FLOPS = 2 * (2 * K * R * J + NF * R * J + R * N * O)

F32 = mybir.dt.float32
BF16 = mybir.dt.bfloat16
I32 = mybir.dt.int32
U32 = mybir.dt.uint32
U16 = mybir.dt.uint16
U8 = mybir.dt.uint8
E4 = mybir.dt.float8_e4m3fn_x4
E5 = mybir.dt.float8_e5m2_x4
E2 = mybir.dt.float4_e2m1fn_x4
ALU = mybir.AluOpType
COPY = mybir.ActivationFunctionType.Copy
ABS = mybir.ActivationFunctionType.Abs
P = 128
PACK = 4


def tile_list_ownanswer_leaned_one_ownpage_kernel(
    tc, xt_words, xt_scales, xo_words, xo_scales, w_words, w_scales, w2_words, w2_scales, w0_words, w0_scales,
    sa, sb, wb_words, wb_scales, offs, offs2, offs3, offs4, offs5, offs6, offs7, out):
    nc = tc.nc
    with ExitStack() as ctx:
        sb_pool = ctx.enter_context(tc.tile_pool(name="keep", bufs=1))
        psum = ctx.enter_context(tc.psum_pool(name="psum", bufs=1))

        def sbuf(name, shape, dtype, tag=""):
            return sb_pool.tile(shape, dtype, name=name, tag=tag or name, align_bytes=64)

        def load_list(name, src):
            lst = sb_pool.tile(list(src.shape), U16, name=name)
            nc.sync.dma_start(lst[:], src)
            return lst

        def plane(name, cols, engine=nc.vector):
            pl = sbuf(name, [P, cols], U8)
            engine.memset(pl[:].bitcast(I32), 0)
            return pl

        def load_plane(pl, src, queues):
            for q in range(4):
                queues[q].dma_start(pl[32 * q:32 * q + 4, :].bitcast(I32), src[0, 4 * q:4 * q + 4, :].bitcast(I32))

        def folded(name, cols, engine=nc.vector):
            pl = sbuf(name, [P, 2 * cols], U8)
            engine.memset(pl[0:64, :].bitcast(I32), 0)
            return pl

        def load_folded(pl, src, queue=nc.sync, row=0):
            rows = src[0].bitcast(I32).rearrange("(u q r) c -> q r u c", u=2, q=2)
            for q in range(2):
                queue.dma_start(pl[32 * q + row:32 * q + row + 4, :].bitcast(I32).rearrange("r (u c) -> r u c", u=2), rows[q])

        def unfold(pl):
            cols = pl.shape[1] // 2
            nc.vector.tensor_copy(pl[64:128, 0:cols].bitcast(I32), pl[0:64, cols:2 * cols].bitcast(I32))

        def load_words(name, src, nbytes):
            tl = sbuf(name, [P, nbytes // 4], I32)
            nc.sync.dma_start(tl[:], src.bitcast(I32))
            return tl

        def flat(words):
            return words[0].rearrange("p n t -> p (n t)")

        w_pl = folded("w_pl", R, nc.gpsimd)
        xt_pl = plane("xt_pl", T)
        xo_pl = plane("xo_pl", Z)
        b_pl = folded("b_pl", R)
        wb_pl = plane("wb_pl", N)
        board = [sbuf("board%d" % i, [P, C], F32) for i in range(2)]
        for bd in board:
            nc.gpsimd.memset(bd[:], 0.0)

        l1 = load_list("l1", offs)
        w_w = load_words("w_w", w_words[0], 2 * R)
        xt_w = load_words("xt_w", flat(xt_words), 4 * T)
        load_folded(w_pl, w_scales, nc.scalar)
        load_plane(xt_pl, xt_scales, [nc.scalar, nc.scalar, nc.sync, nc.sync])
        l3 = load_list("l3", offs3)
        l2 = load_list("l2", offs2)
        load_plane(xo_pl, xo_scales, [nc.sync] * 4)
        xo_w = load_words("xo_w", flat(xo_words), 4 * Z)
        w2_w = load_words("w2_w", flat(w2_words), 4 * R)
        w0_w = load_words("w0_w", flat(w0_words), 4 * R)
        load_folded(b_pl, w2_scales)
        load_folded(b_pl, w0_scales, row=4)
        l4 = load_list("l4", offs4)
        sa_t = sbuf("sa_t", [P, PACK], F32)
        nc.sync.dma_start(sa_t[:], sa.rearrange("(p t) o -> p (t o)", t=PACK))
        l5 = load_list("l5", offs5)
        l6 = load_list("l6", offs6)
        sb_t = sbuf("sb_t", [P, PACK], F32)
        nc.sync.dma_start(sb_t[:], sb.rearrange("(p t) o -> p (t o)", t=PACK))
        wb_w = load_words("wb_w", wb_words[0], 2 * N)
        load_plane(wb_pl, wb_scales, [nc.sync] * 4)
        l7 = load_list("l7", offs7)

        xt_gs = sbuf("xt_gs", [P, J], U8)
        xt_g = sbuf("xt_g", [P, J], U32)
        HALF = J // 2

        def half_cols(h):
            return slice(HALF * h, HALF * (h + 1))

        def half_list(lst, h):
            return lst[:, HALF // 16 * h:HALF // 16 * (h + 1)]

        def pick_scales(h):
            nc.vector.tensor_copy(xt_gs[:, half_cols(h)], xt_pl[:].indirect(half_list(l1, h)))

        def pick_words(h):
            nc.vector.tensor_copy(xt_g[:, half_cols(h)], xt_w[:].bitcast(U32).indirect(half_list(l1, h)))

        w_d = sbuf("w_d", [P, PACK, P], U16)
        w_ds = [sbuf("w_ds0", [P, 2, P], U8), sbuf("w_ds1", [P, 2, P], U8, "xt_pl")]

        def deal_w_scales(u):
            nc.vector.tensor_copy(w_ds[u][:], w_pl[:, 0:R].rearrange("p (m t) -> p t m", t=PACK)[:, 2 * u:2 * u + 2, :])

        nc.scalar.copy(w_d[:], w_w[:].bitcast(U16).rearrange("p (m t) -> p t m", t=PACK))
        unfold(w_pl)
        deal_w_scales(0)

        a_sb = [sbuf("a_sb%d" % t, [P, J], F32) for t in range(PACK)]

        def first(t, cols, bank, copy):
            a_ps = psum.tile([P, cols.stop - cols.start], F32, name="a_ps", tag="bank%d" % bank)
            nc.tensor.matmul_mx(a_ps[:], lhsT=w_d[:, t, :].bitcast(E2), lhsT_scale=w_ds[t // 2][:, t % 2, :],
                                rhs=xt_g[:, cols].bitcast(E5), rhs_scale=xt_gs[:, cols], start=True, stop=True)
            copy(a_sb[t][:, cols], a_ps[:])

        def put_half(t, h):
            nc.scalar.activation(board[t % 2][:].indirect(half_list(l3, h)), a_sb[t][:, half_cols(h)], COPY)

        pick_words(0)
        pick_scales(0)
        first(0, half_cols(0), 0, nc.scalar.copy)
        put_half(0, 0)
        first(1, half_cols(0), 1, nc.vector.tensor_copy)
        put_half(1, 0)
        pick_words(1)
        pick_scales(1)
        first(0, half_cols(1), 2, nc.vector.tensor_copy)
        put_half(0, 1)
        first(1, half_cols(1), 3, nc.vector.tensor_copy)
        put_half(1, 1)
        deal_w_scales(1)
        for t in range(2, PACK):
            first(t, slice(0, J), t - 2, nc.vector.tensor_copy)

        xo_gs = sbuf("xo_gs", [P, J], U8)
        nc.vector.tensor_copy(xo_gs[:], xo_pl[:].indirect(l2[:]))
        xo_g = sbuf("xo_g", [P, J], U32)
        nc.vector.tensor_copy(xo_g[:], xo_w[:].bitcast(U32).indirect(l2[:]))

        def deal(name, words):
            d = sbuf(name + "_d", [P, PACK, P], I32)
            nc.vector.tensor_copy(d[:], words[:].rearrange("p (m t) -> p t m", t=PACK))
            return d

        w2_d = deal("w2", w2_w)
        w0_d = deal("w0", w0_w)
        unfold(b_pl)
        b_ds = sbuf("b_ds", [P, PACK, P], U8)
        nc.vector.tensor_copy(b_ds[:], b_pl[:, 0:R].rearrange("p (m t) -> p t m", t=PACK))
        b_ps = [psum.tile([P, J], F32, name="b_ps%d" % t, tag="bank%d" % (4 + t)) for t in range(PACK)]
        for t in range(PACK):
            nc.tensor.matmul_mx(b_ps[t][:], lhsT=w2_d[:, t, :].bitcast(E4), lhsT_scale=b_ds[:, t, :],
                                rhs=xt_g[:].bitcast(E5), rhs_scale=xt_gs[:], start=True, stop=False)
            nc.tensor.matmul_mx(b_ps[t][:], lhsT=w0_d[:, t, :].bitcast(E4), lhsT_scale=b_ds[4:P, t, :],
                                rhs=xo_g[:].bitcast(E4), rhs_scale=xo_gs[:], start=False, stop=True)

        pages = [sbuf("page%d" % i, [P, E], F32, tag) for i, tag in enumerate(("xo_w", "w2_w"))]
        for pg in pages:
            nc.gpsimd.memset(pg[:], 0.0)

        look = [sbuf("look%d" % t, [P, J], F32) for t in range(PACK)]
        rb = [sbuf("rb%d" % t, [P, J], F32) for t in range(PACK)]
        plain = sbuf("plain", [P, PACK, O], F32)
        leaned = sbuf("leaned", [P, PACK, O], F32)
        OH = O // 2

        def places(h):
            return slice(OH * h, OH * (h + 1))

        def place_list(lst, h):
            return lst[:, OH // 16 * h:OH // 16 * (h + 1)]

        def put(t):
            nc.scalar.activation(board[t % 2][:].indirect(l3[:]), a_sb[t][:], COPY)

        def fetch(t, cols=slice(0, J)):
            offsets = l4[:, cols.start // 16:cols.stop // 16]
            nc.scalar.activation(look[t][:, cols], board[t % 2][:].indirect(offsets), COPY, scale=sa_t[:, t:t + 1])
            nc.vector.tensor_tensor(rb[t][:, cols], look[t][:, cols], b_ps[t][:, cols], ALU.max)

        def pick(t, cols, offsets5, offsets6):
            nc.scalar.activation(leaned[:, t, cols], rb[t][:].indirect(offsets6), COPY, scale=sb_t[:, t:t + 1])
            nc.vector.tensor_copy(plain[:, t, cols], rb[t][:].indirect(offsets5))

        fetch(0)
        fetch(1)
        put(2)
        put(3)
        fetch(2)
        fetch(3, half_cols(0))
        fetch(3, half_cols(1))
        for t in range(PACK - 1):
            pick(t, slice(0, O), l5[:], l6[:])
        for h in range(2):
            pick(PACK - 1, places(h), place_list(l5, h), place_list(l6, h))

        hq = sbuf("hq", [P, 3 * OH], U32)
        hs = sbuf("hs", [P, 3 * OH], U8)
        nc.vector.memset(hq[:, OH:2 * OH].bitcast(I32), 0)
        nc.vector.memset(hs[:, OH:2 * OH].bitcast(I32), 0)
        diff = [sbuf("diff%d" % h, [P, PACK, OH], F32) for h in range(2)]
        hid = [sbuf("hid%d" % h, [P, OH, PACK], BF16) for h in range(2)]
        for h in range(2):
            nc.vector.tensor_tensor(diff[h][:], plain[:, :, places(h)], leaned[:, :, places(h)], ALU.subtract)
            nc.scalar.activation(hid[h][:], diff[h][:].rearrange("p t o -> p o t"), ABS)
        for h in range(2):
            made = slice(2 * OH * h, 2 * OH * h + OH)
            read = slice(OH * h, OH * h + O)
            nc.vector.quantize_mx(hq[:, made].bitcast(E4), hs[:, made], hid[h][:].rearrange("p o t -> p (o t)"))
            for i in range(2):
                p_ps = psum.tile([P, O], F32, name="p_ps", tag="bank%d" % (2 * h + i))
                nc.tensor.matmul_mx(p_ps[:], lhsT=wb_w[:].bitcast(U8)[:, 2 * P * i:2 * P * (i + 1)].bitcast(E2),
                                    lhsT_scale=wb_pl[:, P * i:P * (i + 1)], rhs=hq[:, read].bitcast(E4), rhs_scale=hs[:, read],
                                    start=True, stop=True)
                p_sb = sbuf("p_sb%d%d" % (h, i), [P, OH], F32)
                nc.vector.tensor_copy(p_sb[:], p_ps[:, places(h)])
                nc.scalar.activation(pages[i][:].indirect(place_list(l7, h)), p_sb[:], COPY)
        for i in range(2):
            nc.sync.dma_start(out[P * i:P * (i + 1), :], pages[i][:])
